import numpy as np
import ml_dtypes

BF16 = ml_dtypes.bfloat16


def bf(x):
    return np.asarray(x, np.float32).astype(BF16)


def f32(x):
    return np.asarray(x, np.float32)


def f64(x):
    return np.asarray(x).astype(np.float64)


def striped(idx):
    return np.tile(idx.reshape(-1, 16).T, (8, 1))


S, K, M, N, D, V = 4096, 256, 128, 3072, 2, 1536


def setup_inputs():
    return {"table": bf(np.random.standard_normal((K, S))), "w": bf(np.random.standard_normal((K, M)) / np.sqrt(D * K)), "b": f32(0.5 * np.random.standard_normal((M, 1))), "offs": striped(np.random.permutation(np.tile(np.arange(S), 2))[:N])}


def reference(table, w, b, offs):
    idx = offs[:16].T.reshape(-1)
    x = f64(table)[:, idx]
    y = f64(w).T @ sum(x[:, t * V : (t + 1) * V] for t in range(D))
    return np.maximum(y + f64(b), 0.0)

@@ -1,0 +1,55 @@
+import concourse.mybir as mybir
+
+BF16, F32, U16 = mybir.dt.bfloat16, mybir.dt.float32, mybir.dt.uint16
+ADD, MAX = mybir.AluOpType.add, mybir.AluOpType.max
+
+P = 128
+NODES = 4096
+FEATURES = 256
+BLOCKS = FEATURES // P
+M = 128
+NEIGHBOURS = 2
+V = 1536
+BANK = 512
+BANKS = V // BANK
+PER_COLUMN = 16
+
+FLOPS = 2 * FEATURES * M * V + (NEIGHBOURS - 1) * FEATURES * V
+
+
+def tile_gather_matmul_kernel(tc, table, w, b, offs, out):
+    nc = tc.nc
+    with (
+        tc.tile_pool(name="held", bufs=1) as held,
+        tc.psum_pool(name="psum", bufs=1) as psum,
+    ):
+        offsets = held.tile([P, NEIGHBOURS * V // PER_COLUMN], U16, name="offsets")
+        nc.sync.dma_start(offsets[:], offs)
+        windows = []
+        for kb in range(BLOCKS):
+            window = held.tile([P, NODES], BF16, name=f"window{kb}")
+            nc.sync.dma_start(window[:], table[kb * P : (kb + 1) * P, :])
+            windows.append(window)
+        weights = held.tile([P, BLOCKS, M], BF16, name="weights")
+        nc.scalar.dma_start(weights[:], w.rearrange("(kb p) m -> p kb m", p=P))
+        bias = held.tile([P, 1], F32, name="bias")
+        nc.scalar.dma_start(bias[:], b)
+
+        banks = [psum.tile([P, BANK], F32, name=f"bank{j}") for j in range(BANKS)]
+        for kb in range(BLOCKS):
+            for j in range(BANKS):
+                for t in range(NEIGHBOURS):
+                    first = (t * V + j * BANK) // PER_COLUMN
+                    piece = offsets[:, first : first + BANK // PER_COLUMN]
+                    nc.tensor.matmul(
+                        banks[j][:],
+                        weights[:, kb, :],
+                        windows[kb][:].indirect(piece),
+                        start=(kb == 0 and t == 0),
+                        stop=(kb == BLOCKS - 1 and t == NEIGHBOURS - 1),
+                    )
+
+        for j in range(BANKS):
+            result = held.tile([P, BANK], F32, name=f"result{j}")
+            nc.vector.tensor_scalar(result[:], banks[j][:], bias[:, 0:1], 0.0, ADD, MAX)
+            nc.sync.dma_start(out[:, j * BANK : (j + 1) * BANK], result[:])

@@ -13,6 +13,7 @@ V = 1536
 BANK = 512
 BANKS = V // BANK
 PER_COLUMN = 16
+WARM_UPS = 10
 
 FLOPS = 2 * FEATURES * M * V + (NEIGHBOURS - 1) * FEATURES * V
 
@@ -34,6 +35,12 @@ def tile_gather_matmul_kernel(tc, table, w, b, offs, out):
         nc.scalar.dma_start(weights[:], w.rearrange("(kb p) m -> p kb m", p=P))
         bias = held.tile([P, 1], F32, name="bias")
         nc.scalar.dma_start(bias[:], b)
+
+        zeros = held.tile([P, BANK], BF16, name="zeros")
+        nc.vector.memset(zeros[:], 0.0)
+        unread = psum.tile([P, BANK], F32, name="unread")
+        for i in range(WARM_UPS):
+            nc.tensor.matmul(unread[:], zeros[:, 0:M], zeros[:], start=True, stop=True)
 
         banks = [psum.tile([P, BANK], F32, name=f"bank{j}") for j in range(BANKS)]
         for kb in range(BLOCKS):

@@ -5,6 +5,7 @@ ADD, MAX = mybir.AluOpType.add, mybir.AluOpType.max
 
 P = 128
 NODES = 4096
+HALF = NODES // 2
 FEATURES = 256
 BLOCKS = FEATURES // P
 M = 128
@@ -13,7 +14,6 @@ V = 1536
 BANK = 512
 BANKS = V // BANK
 PER_COLUMN = 16
-WARM_UPS = 10
 
 FLOPS = 2 * FEATURES * M * V + (NEIGHBOURS - 1) * FEATURES * V
 
@@ -29,18 +29,14 @@ def tile_gather_matmul_kernel(tc, table, w, b, offs, out):
         windows = []
         for kb in range(BLOCKS):
             window = held.tile([P, NODES], BF16, name=f"window{kb}")
-            nc.sync.dma_start(window[:], table[kb * P : (kb + 1) * P, :])
+            rows = table[kb * P : (kb + 1) * P, :]
+            nc.sync.dma_start(window[:, 0:HALF], rows[:, 0:HALF])
+            nc.scalar.dma_start(window[:, HALF:NODES], rows[:, HALF:NODES])
             windows.append(window)
         weights = held.tile([P, BLOCKS, M], BF16, name="weights")
-        nc.scalar.dma_start(weights[:], w.rearrange("(kb p) m -> p kb m", p=P))
+        nc.gpsimd.dma_start(weights[:], w.rearrange("(kb p) m -> p kb m", p=P))
         bias = held.tile([P, 1], F32, name="bias")
-        nc.scalar.dma_start(bias[:], b)
-
-        zeros = held.tile([P, BANK], BF16, name="zeros")
-        nc.vector.memset(zeros[:], 0.0)
-        unread = psum.tile([P, BANK], F32, name="unread")
-        for i in range(WARM_UPS):
-            nc.tensor.matmul(unread[:], zeros[:, 0:M], zeros[:], start=True, stop=True)
+        nc.gpsimd.dma_start(bias[:], b)
 
         banks = [psum.tile([P, BANK], F32, name=f"bank{j}") for j in range(BANKS)]
         for kb in range(BLOCKS):

@@ -5,7 +5,6 @@ ADD, MAX = mybir.AluOpType.add, mybir.AluOpType.max
 
 P = 128
 NODES = 4096
-HALF = NODES // 2
 FEATURES = 256
 BLOCKS = FEATURES // P
 M = 128
@@ -29,14 +28,12 @@ def tile_gather_matmul_kernel(tc, table, w, b, offs, out):
         windows = []
         for kb in range(BLOCKS):
             window = held.tile([P, NODES], BF16, name=f"window{kb}")
-            rows = table[kb * P : (kb + 1) * P, :]
-            nc.sync.dma_start(window[:, 0:HALF], rows[:, 0:HALF])
-            nc.scalar.dma_start(window[:, HALF:NODES], rows[:, HALF:NODES])
+            nc.sync.dma_start(window[:], table[kb * P : (kb + 1) * P, :])
             windows.append(window)
         weights = held.tile([P, BLOCKS, M], BF16, name="weights")
-        nc.gpsimd.dma_start(weights[:], w.rearrange("(kb p) m -> p kb m", p=P))
+        nc.scalar.dma_start(weights[:], w.rearrange("(kb p) m -> p kb m", p=P))
         bias = held.tile([P, 1], F32, name="bias")
-        nc.gpsimd.dma_start(bias[:], b)
+        nc.scalar.dma_start(bias[:], b)
 
         banks = [psum.tile([P, BANK], F32, name=f"bank{j}") for j in range(BANKS)]
         for kb in range(BLOCKS):
@@ -52,7 +49,12 @@ def tile_gather_matmul_kernel(tc, table, w, b, offs, out):
                         stop=(kb == BLOCKS - 1 and t == NEIGHBOURS - 1),
                     )
 
+        result = held.tile([P, V], F32, name="result")
         for j in range(BANKS):
-            result = held.tile([P, BANK], F32, name=f"result{j}")
-            nc.vector.tensor_scalar(result[:], banks[j][:], bias[:, 0:1], 0.0, ADD, MAX)
-            nc.sync.dma_start(out[:, j * BANK : (j + 1) * BANK], result[:])
+            for h, queue in enumerate((nc.sync, nc.scalar)):
+                low = h * (BANK // 2)
+                columns = slice(j * BANK + low, j * BANK + low + BANK // 2)
+                nc.vector.tensor_scalar(
+                    result[:, columns], banks[j][:, low : low + BANK // 2], bias[:, 0:1], 0.0, ADD, MAX
+                )
+                queue.dma_start(out[:, columns], result[:, columns])

@@ -1,7 +1,7 @@
 import concourse.mybir as mybir
 
 BF16, F32, U16 = mybir.dt.bfloat16, mybir.dt.float32, mybir.dt.uint16
-ADD, MAX = mybir.AluOpType.add, mybir.AluOpType.max
+RELU = mybir.ActivationFunctionType.Relu
 
 P = 128
 NODES = 4096
@@ -49,12 +49,7 @@ def tile_gather_matmul_kernel(tc, table, w, b, offs, out):
                         stop=(kb == BLOCKS - 1 and t == NEIGHBOURS - 1),
                     )
 
-        result = held.tile([P, V], F32, name="result")
         for j in range(BANKS):
-            for h, queue in enumerate((nc.sync, nc.scalar)):
-                low = h * (BANK // 2)
-                columns = slice(j * BANK + low, j * BANK + low + BANK // 2)
-                nc.vector.tensor_scalar(
-                    result[:, columns], banks[j][:, low : low + BANK // 2], bias[:, 0:1], 0.0, ADD, MAX
-                )
-                queue.dma_start(out[:, columns], result[:, columns])
+            result = held.tile([P, BANK], F32, name=f"result{j}")
+            nc.scalar.activation(result[:], banks[j][:], RELU, bias=bias[:, 0:1])
+            nc.scalar.dma_start(out[:, j * BANK : (j + 1) * BANK], result[:])

import concourse.mybir as mybir

BF16, F32, U16 = mybir.dt.bfloat16, mybir.dt.float32, mybir.dt.uint16
RELU = mybir.ActivationFunctionType.Relu

P = 128
NODES = 4096
FEATURES = 256
BLOCKS = FEATURES // P
M = 128
NEIGHBOURS = 2
V = 1536
BANK = 512
BANKS = V // BANK
PER_COLUMN = 16

FLOPS = 2 * FEATURES * M * V + (NEIGHBOURS - 1) * FEATURES * V


def tile_gather_matmul_kernel(tc, table, w, b, offs, out):
    nc = tc.nc
    with (
        tc.tile_pool(name="held", bufs=1) as held,
        tc.psum_pool(name="psum", bufs=1) as psum,
    ):
        offsets = held.tile([P, NEIGHBOURS * V // PER_COLUMN], U16, name="offsets")
        nc.sync.dma_start(offsets[:], offs)
        windows = []
        for kb in range(BLOCKS):
            window = held.tile([P, NODES], BF16, name=f"window{kb}")
            nc.sync.dma_start(window[:], table[kb * P : (kb + 1) * P, :])
            windows.append(window)
        weights = held.tile([P, BLOCKS, M], BF16, name="weights")
        nc.scalar.dma_start(weights[:], w.rearrange("(kb p) m -> p kb m", p=P))
        bias = held.tile([P, 1], F32, name="bias")
        nc.scalar.dma_start(bias[:], b)

        banks = [psum.tile([P, BANK], F32, name=f"bank{j}") for j in range(BANKS)]
        for kb in range(BLOCKS):
            for j in range(BANKS):
                for t in range(NEIGHBOURS):
                    first = (t * V + j * BANK) // PER_COLUMN
                    piece = offsets[:, first : first + BANK // PER_COLUMN]
                    nc.tensor.matmul(
                        banks[j][:],
                        weights[:, kb, :],
                        windows[kb][:].indirect(piece),
                        start=(kb == 0 and t == 0),
                        stop=(kb == BLOCKS - 1 and t == NEIGHBOURS - 1),
                    )

        for j in range(BANKS):
            result = held.tile([P, BANK], F32, name=f"result{j}")
            nc.scalar.activation(result[:], banks[j][:], RELU, bias=bias[:, 0:1])
            nc.scalar.dma_start(out[:, j * BANK : (j + 1) * BANK], result[:])
